import numpy as np
import ml_dtypes


def mxq(x, axis, fmt="e4m3"):
    dtype, down = {"e4m3": (ml_dtypes.float8_e4m3fn, 7), "e5m2": (ml_dtypes.float8_e5m2, 14)}[fmt]
    v = np.moveaxis(np.asarray(x, np.float32).astype(ml_dtypes.bfloat16).astype(np.float64), axis, -1)
    blocks = v.reshape(v.shape[:-1] + (-1, 32))
    amax = np.abs(blocks).max(-1, keepdims=True)
    byte = np.maximum(np.where(amax > 0, np.frexp(amax)[1] - 1 + 127, 0) - down, 1)
    scale = np.exp2(byte - 127.0)
    codes = (blocks / scale).astype(np.float32).astype(dtype).astype(np.float64)
    return np.moveaxis((codes * scale).reshape(v.shape), -1, axis)


WIDE = False


def mx_kscale(k):
    if not WIDE:
        return np.ones(k)
    levels = np.array([10, -10, 5, -5, 0])
    if k % 512:
        return np.exp2(np.random.permutation(np.resize(levels, k // 32))).repeat(32)
    a = np.empty((k // 512, 16))
    for p in range(k // 512):
        a[p, :8] = np.random.permutation(np.resize(levels, 8))
        for g in range(8):
            far = levels[np.abs(levels - a[p, g]) >= 10]
            a[p, g + 8] = far[np.random.randint(len(far))]
    return np.exp2(a.ravel()).repeat(32)


def f64(x):
    return np.asarray(x).astype(np.float64)


def striped8(idx):
    return np.asarray(idx).reshape(8, -1, 16).transpose(0, 2, 1).reshape(128, -1).astype(np.uint16)


def unstriped8(offs):
    return offs.reshape(8, 16, -1).transpose(0, 2, 1).reshape(8, -1).astype(np.int64)


def pick8(x, idx, run):
    r = np.arange(len(x))
    return x[r[:, None], idx[r % (8 * run) // run]]


E2M1 = np.array([0.0, 0.5, 1.0, 1.5, 2.0, 3.0, 4.0, 6.0, -0.0, -0.5, -1.0, -1.5, -2.0, -3.0, -4.0, -6.0])


def pack_weight(w, fmt):
    k, n = w.shape
    w = f64(np.asarray(w, np.float32).astype(ml_dtypes.bfloat16)).reshape(k // 32, 32, n)
    amax = np.abs(w).max(1)
    if fmt == "e4m3":
        byte = np.frexp(amax)[1] - 1 + 127 - 7
    else:
        mant, ex = np.frexp(amax / 6.0)
        byte = np.where(mant > 0.5, ex, ex - 1) + 127
    byte = np.clip(np.where(amax > 0, byte, 1), 1, 254)
    scaled = (w * np.exp2(127.0 - byte)[:, None, :]).reshape(k, n).astype(np.float32)
    by_word = np.ascontiguousarray(scaled.reshape(k // 512, 128, 4, n).transpose(0, 1, 3, 2))
    if fmt == "e4m3":
        words = by_word.astype(ml_dtypes.float8_e4m3fn).view(np.uint8)
    else:
        c = by_word.astype(ml_dtypes.float4_e2m1fn).view(np.uint8) & 0xF
        words = (c[..., 0::2] | (c[..., 1::2] << 4)).reshape(k // 512, 128, 2 * n)
    return np.ascontiguousarray(words), np.ascontiguousarray(byte.astype(np.uint8).reshape(k // 512, 16, n))


def unpack_weight(words, scales, fmt):
    g, _, n = scales.shape
    words = np.ascontiguousarray(words).reshape(g, 128, n, -1)
    if fmt == "e4m3":
        vals = words.view(ml_dtypes.float8_e4m3fn).astype(np.float64)
    else:
        nib = np.empty((g, 128, n, 4), np.uint8)
        nib[..., 0::2] = words & 0xF
        nib[..., 1::2] = words >> 4
        vals = E2M1[nib]
    vals = vals * np.repeat(np.exp2(scales.astype(np.float64) - 127.0), 8, axis=1)[..., None]
    return vals.transpose(0, 1, 3, 2).reshape(g * 512, n)


D, V, Q, I = 512, 2048, 128, 512


def setup_inputs():
    n = np.random.standard_normal
    idx = np.stack([np.random.permutation(V)[:I] for _ in range(8)])
    idx2 = np.stack([np.random.permutation(V)[:I] for _ in range(8)])
    fd = mx_kscale(D)
    vocp = pack_weight(n((D, V)) / fd[:, None], "e2m1")
    return {
        "hid": (n((D, Q)) * 1.0 / np.sqrt(D) * fd[:, None]).astype(np.float32),
        "voc_words": vocp[0],
        "voc_scales": vocp[1],
        "stake": (np.random.uniform(0.5, 2.0, (Q, 1))).astype(np.float32),
        "old": (0.5 * n((Q, V))).astype(np.float32),
        "offs": striped8(idx),
        "offs2": striped8(idx2),
    }


def reference(hid, voc_words, voc_scales, stake, old, offs, offs2):
    idx = unstriped8(offs)
    idx2 = unstriped8(offs2)
    vocu = unpack_weight(voc_words, voc_scales, "e2m1")
    hidq = mxq(f64(hid), 0, "e4m3")
    a = hidq.T @ vocu
    m1 = np.max(a, axis=1, keepdims=True)
    p = np.exp(a - m1)
    z = np.sum(p, axis=1, keepdims=True)
    px = np.exp(pick8(a, idx, 16) - m1)
    px2 = np.exp(pick8(a, idx2, 16) - m1)
    ma = np.sum(px, axis=1, keepdims=True) / z
    mb = np.sum(px2, axis=1, keepdims=True) / z
    dmb = f64(stake) / (ma * mb * 16.0 + 1.0) * 16.0 * ma
    dma = f64(stake) / (ma * mb * 16.0 + 1.0) * 16.0 * mb
    dpx2 = dmb / z
    dpx = dma / z
    dz = dmb * np.sum(px2, axis=1, keepdims=True) / np.square(z) * (-1.0) - dma * np.sum(px, axis=1, keepdims=True) / np.square(z)
    e1 = dpx2 * px2
    s1 = np.zeros((Q, V))
    s1[np.arange(Q)[:, None], idx2[np.arange(Q) % 128 // 16]] = e1
    e2 = dpx * px
    s2 = np.zeros((Q, V))
    s2[np.arange(Q)[:, None], idx[np.arange(Q) % 128 // 16]] = e2
    da = dz * p + s1 + s2
    y = da * 512.0 + f64(old)
    return y

@@ -1,0 +1,173 @@
+from contextlib import ExitStack
+
+import concourse.mybir as mybir
+
+D, V, Q, LISTED = 512, 2048, 128, 512
+FLOPS = 2 * D * V * Q
+
+F32 = mybir.dt.float32
+BF16 = mybir.dt.bfloat16
+I32 = mybir.dt.int32
+U32 = mybir.dt.uint32
+U16 = mybir.dt.uint16
+U8 = mybir.dt.uint8
+FP8X4 = mybir.dt.float8_e4m3fn_x4
+FP4X4 = mybir.dt.float4_e2m1fn_x4
+ALU = mybir.AluOpType
+ACT = mybir.ActivationFunctionType
+AX = mybir.AxisListType
+
+P = 128
+PACK = 4
+BANK = 512
+BANKS = V // BANK
+
+
+def tile_attend_bjointcover_heads_kernel(tc, hid, voc_words, voc_scales, stake, old, offs, offs2, out):
+    nc = tc.nc
+    with ExitStack() as ctx:
+        keep = ctx.enter_context(tc.tile_pool(name="keep", bufs=1))
+        ring = ctx.enter_context(tc.tile_pool(name="ring", bufs=4))
+        psum = ctx.enter_context(tc.psum_pool(name="psum", bufs=1))
+
+        planes = keep.tile([P, V], U8, align_bytes=64)
+        nc.vector.memset(planes[:].bitcast(U32), 0)
+
+        hid_raw = keep.tile([P, PACK, Q], F32, tag="staging")
+        nc.sync.dma_start(out=hid_raw[:], in_=hid.rearrange("(p t) q -> p t q", t=PACK))
+        for quad in range(4):
+            nc.scalar.dma_start(
+                out=planes[32 * quad : 32 * quad + 4, :].bitcast(I32),
+                in_=voc_scales[0, 4 * quad : 4 * quad + 4, :].bitcast(I32),
+            )
+        words = keep.tile([P, 2 * V], U8, align_bytes=64)
+        nc.sync.dma_start(out=words[:].bitcast(I32), in_=voc_words[0].bitcast(I32))
+        list_a = keep.tile([P, LISTED // 16], U16)
+        nc.sync.dma_start(out=list_a[:], in_=offs)
+        list_b = keep.tile([P, LISTED // 16], U16)
+        nc.sync.dma_start(out=list_b[:], in_=offs2)
+
+        placed_b = keep.tile([P, V], F32)
+        nc.vector.memset(placed_b[:], 0.0)
+        stake_sb = keep.tile([P, 1], F32)
+        nc.gpsimd.dma_start(out=stake_sb[:], in_=stake)
+
+        grouped = keep.tile([P, Q, PACK], BF16, align_bytes=64, tag="grouped")
+        nc.vector.tensor_copy(
+            out=grouped[:].rearrange("p (c i) t -> p c t i", i=4),
+            in_=hid_raw[:].rearrange("p t (c i) -> p c t i", i=4),
+        )
+        codes = keep.tile([P, Q], U32, align_bytes=64)
+        hid_plane = keep.tile([P, Q], U8, align_bytes=64)
+        nc.vector.quantize_mx(
+            out=codes[:].bitcast(FP8X4), scales=hid_plane[:], in_=grouped[:].rearrange("p q t -> p (q t)")
+        )
+
+        old_sb = keep.tile([P, V], F32, tag="staging")
+        nc.sync.dma_start(out=old_sb[:], in_=old)
+        placed_a = keep.tile([P, V], F32, align_bytes=64, tag="grouped")
+        nc.gpsimd.memset(placed_a[:], 0.0)
+
+        a = keep.tile([P, V], F32)
+        p = keep.tile([P, V], F32)
+        bank_max = keep.tile([P, BANKS], F32)
+        bank_neg = keep.tile([P, BANKS], F32)
+        bank_sum = keep.tile([P, BANKS], F32)
+        for k in range(BANKS):
+            cols = slice(k * BANK, (k + 1) * BANK)
+            acc = psum.tile([P, BANK], F32, name=f"acc{k}")
+            nc.tensor.matmul_mx(
+                out=acc[:],
+                lhsT=codes[:].bitcast(FP8X4),
+                lhsT_scale=hid_plane[:],
+                rhs=words[:, 2 * k * BANK : 2 * (k + 1) * BANK].bitcast(FP4X4),
+                rhs_scale=planes[:, cols],
+                start=True,
+                stop=True,
+            )
+            nc.vector.tensor_scalar(
+                out=a[:, cols], in0=acc[:], scalar1=1.0, scalar2=None, op0=ALU.mult, op1=ALU.max,
+                accum_out=bank_max[:, k : k + 1],
+            )
+            nc.scalar.mul(bank_neg[:, k : k + 1], bank_max[:, k : k + 1], -1.0)
+            nc.scalar.activation(
+                out=p[:, cols], in_=a[:, cols], func=ACT.Exp, bias=bank_neg[:, k : k + 1],
+                accum_out=bank_sum[:, k : k + 1],
+            )
+
+        got_a = keep.tile([P, LISTED], F32)
+        nc.vector.tensor_copy(out=got_a[:], in_=a[:].indirect(list_a[:]))
+        neg_max = keep.tile([P, 1], F32)
+        nc.vector.tensor_reduce(out=neg_max[:], in_=bank_max[:], axis=AX.X, op=ALU.max, negate=True)
+        got_b = keep.tile([P, LISTED], F32)
+        nc.vector.tensor_copy(out=got_b[:], in_=a[:].indirect(list_b[:]))
+
+        px_a = keep.tile([P, LISTED], F32)
+        sum_a = keep.tile([P, 1], F32)
+        nc.scalar.activation(out=px_a[:], in_=got_a[:], func=ACT.Exp, bias=neg_max[:], accum_out=sum_a[:])
+        rebase = keep.tile([P, BANKS], F32)
+        nc.scalar.activation(out=rebase[:], in_=bank_max[:], func=ACT.Exp, bias=neg_max[:])
+        coef = keep.tile([P, 1 + BANKS], F32)
+        nc.scalar.mul(coef[:, 0:1], stake_sb[:], 512.0)
+        h = keep.tile([P, 1], F32)
+        nc.scalar.activation(out=h[:], in_=sum_a[:], func=ACT.Copy, scale=coef[:, 0:1])
+        px_b = keep.tile([P, LISTED], F32)
+        sum_b = keep.tile([P, 1], F32)
+        nc.scalar.activation(out=px_b[:], in_=got_b[:], func=ACT.Exp, bias=neg_max[:], accum_out=sum_b[:])
+
+        z_parts = keep.tile([P, BANKS], F32)
+        z = keep.tile([P, 1], F32)
+        nc.vector.scalar_tensor_tensor(
+            out=z_parts[:], in0=bank_sum[:], scalar=1.0, in1=rebase[:], op0=ALU.mult, op1=ALU.mult, accum_out=z[:]
+        )
+        zz = keep.tile([P, 1], F32)
+        nc.vector.scalar_tensor_tensor(out=zz[:], in0=z[:], scalar=0.0625, in1=z[:], op0=ALU.mult, op1=ALU.mult)
+        z_inv = keep.tile([P, 1], F32)
+        nc.vector.reciprocal(out=z_inv[:], in_=z[:])
+
+        den = keep.tile([P, 1], F32)
+        nc.vector.tensor_scalar(
+            out=den[:], in0=sum_b[:], scalar1=sum_a[:], scalar2=zz[:], op0=ALU.mult, op1=ALU.add
+        )
+        den_inv = keep.tile([P, 1], F32)
+        nc.vector.reciprocal(out=den_inv[:], in_=den[:])
+        e_b = keep.tile([P, LISTED], F32)
+        nc.vector.tensor_scalar(
+            out=e_b[:], in0=px_b[:], scalar1=h[:], scalar2=den_inv[:], op0=ALU.mult, op1=ALU.mult
+        )
+        nc.vector.tensor_copy(out=placed_b[:].indirect(list_b[:]), in_=e_b[:])
+
+        hz = keep.tile([P, 1], F32)
+        nc.scalar.activation(out=hz[:], in_=h[:], func=ACT.Copy, scale=z_inv[:])
+        hz2 = keep.tile([P, 1], F32)
+        nc.scalar.mul(hz2[:], hz[:], -2.0)
+        nc.scalar.activation(out=coef[:, 1:], in_=rebase[:], func=ACT.Copy, scale=hz2[:])
+        ratio = keep.tile([P, 1], F32)
+        nc.scalar.activation(out=ratio[:], in_=sum_b[:], func=ACT.Copy, scale=den_inv[:])
+        coef2 = keep.tile([P, 1 + BANKS], F32)
+        nc.scalar.activation(out=coef2[:], in_=coef[:], func=ACT.Copy, scale=ratio[:])
+        e_a = keep.tile([P, LISTED], F32)
+        nc.scalar.activation(out=e_a[:], in_=px_a[:], func=ACT.Copy, scale=coef2[:, 0:1])
+        nc.vector.tensor_copy(out=placed_a[:].indirect(list_a[:]), in_=e_a[:])
+
+        dense = []
+        for k in range(BANKS):
+            cols = slice(k * BANK, (k + 1) * BANK)
+            t = ring.tile([P, BANK], F32, name="t")
+            nc.vector.scalar_tensor_tensor(
+                out=t[:], in0=p[:, cols], scalar=coef2[:, 1 + k : 2 + k], in1=old_sb[:, cols],
+                op0=ALU.mult, op1=ALU.add,
+            )
+            dense.append(t)
+        part = []
+        for k in range(BANKS + 1):
+            if k < BANKS:
+                cols = slice(k * BANK, (k + 1) * BANK)
+                w = ring.tile([P, BANK], F32, name="w")
+                nc.vector.tensor_tensor(out=w[:], in0=dense[k][:], in1=placed_b[:, cols], op=ALU.add)
+                part.append(w)
+            if k > 0:
+                cols = slice((k - 1) * BANK, k * BANK)
+                y = ring.tile([P, BANK], F32, name="y")
+                nc.vector.tensor_tensor(out=y[:], in0=part[k - 1][:], in1=placed_a[:, cols], op=ALU.add)
+                nc.sync.dma_start(out=out[:, cols], in_=y[:])

@@ -1,6 +1,7 @@
 from contextlib import ExitStack
 
 import concourse.mybir as mybir
+from concourse.masks import make_identity
 
 D, V, Q, LISTED = 512, 2048, 128, 512
 FLOPS = 2 * D * V * Q
@@ -27,7 +28,6 @@ def tile_attend_bjointcover_heads_kernel(tc, hid, voc_words, voc_scales, stake, 
     nc = tc.nc
     with ExitStack() as ctx:
         keep = ctx.enter_context(tc.tile_pool(name="keep", bufs=1))
-        ring = ctx.enter_context(tc.tile_pool(name="ring", bufs=4))
         psum = ctx.enter_context(tc.psum_pool(name="psum", bufs=1))
 
         planes = keep.tile([P, V], U8, align_bytes=64)
@@ -51,6 +51,9 @@ def tile_attend_bjointcover_heads_kernel(tc, hid, voc_words, voc_scales, stake, 
         nc.vector.memset(placed_b[:], 0.0)
         stake_sb = keep.tile([P, 1], F32)
         nc.gpsimd.dma_start(out=stake_sb[:], in_=stake)
+
+        ident = keep.tile([P, P], F32)
+        make_identity(nc, ident[:])
 
         grouped = keep.tile([P, Q, PACK], BF16, align_bytes=64, tag="grouped")
         nc.vector.tensor_copy(
@@ -142,32 +145,55 @@ def tile_attend_bjointcover_heads_kernel(tc, hid, voc_words, voc_scales, stake, 
         hz2 = keep.tile([P, 1], F32)
         nc.scalar.mul(hz2[:], hz[:], -2.0)
         nc.scalar.activation(out=coef[:, 1:], in_=rebase[:], func=ACT.Copy, scale=hz2[:])
-        ratio = keep.tile([P, 1], F32)
-        nc.scalar.activation(out=ratio[:], in_=sum_b[:], func=ACT.Copy, scale=den_inv[:])
+        coef1 = keep.tile([P, 1 + BANKS], F32)
+        nc.scalar.activation(out=coef1[:], in_=coef[:], func=ACT.Copy, scale=sum_b[:])
         coef2 = keep.tile([P, 1 + BANKS], F32)
-        nc.scalar.activation(out=coef2[:], in_=coef[:], func=ACT.Copy, scale=ratio[:])
+        nc.scalar.activation(out=coef2[:], in_=coef1[:], func=ACT.Copy, scale=den_inv[:])
+        u = keep.tile([P, V], F32)
+        for k in range(BANKS):
+            cols = slice(k * BANK, (k + 1) * BANK)
+            nc.scalar.activation(out=u[:, cols], in_=p[:, cols], func=ACT.Copy, scale=coef2[:, 1 + k : 2 + k])
         e_a = keep.tile([P, LISTED], F32)
         nc.scalar.activation(out=e_a[:], in_=px_a[:], func=ACT.Copy, scale=coef2[:, 0:1])
         nc.vector.tensor_copy(out=placed_a[:].indirect(list_a[:]), in_=e_a[:])
 
-        dense = []
-        for k in range(BANKS):
-            cols = slice(k * BANK, (k + 1) * BANK)
-            t = ring.tile([P, BANK], F32, name="t")
-            nc.vector.scalar_tensor_tensor(
-                out=t[:], in0=p[:, cols], scalar=coef2[:, 1 + k : 2 + k], in1=old_sb[:, cols],
-                op0=ALU.mult, op1=ALU.add,
+        def blocks_of(j):
+            return [3 * j, 3 * j + 1, 3 * j + 2, 12 + j]
+
+        def turn(dst, src, start, stop):
+            nc.tensor.matmul(out=dst, lhsT=src, rhs=ident[:], is_transpose=True, start=start, stop=stop)
+
+        turned = [psum.tile([P, 4, P], F32, name=f"turned{j}") for j in range(4)]
+        place = {b: (j, s) for j in range(4) for s, b in enumerate(blocks_of(j))}
+        for b in range(16):
+            j, s = place[b]
+            turn(turned[j][:, s, :], old_sb[:, b * P : (b + 1) * P], s == 0, False)
+        for b in range(16):
+            j, s = place[b]
+            turn(turned[j][:, s, :], u[:, b * P : (b + 1) * P], False, False)
+
+        sums = []
+        chunks = [[0, 1, 2], [3, 4, 5], [6, 7, 8], [9, 10, 11], [12, 13], [14, 15]]
+        tags = ["acc0", "acc1", "acc2", "acc3", "turned0", "turned1"]
+
+        def finish(c):
+            blocks = chunks[c]
+            back = psum.tile([P, len(blocks), P], F32, name=f"back{c}", tag=tags[c])
+            for i, b in enumerate(blocks):
+                j, s = place[b]
+                turn(back[:, i, :], sums[j][:, s, :], True, True)
+            cols = slice(blocks[0] * P, (blocks[-1] + 1) * P)
+            y = keep.tile([P, len(blocks) * P], F32, name=f"y{c}")
+            nc.vector.tensor_tensor(
+                out=y[:], in0=placed_a[:, cols], in1=back[:].rearrange("p i q -> p (i q)"), op=ALU.add
             )
-            dense.append(t)
-        part = []
-        for k in range(BANKS + 1):
-            if k < BANKS:
-                cols = slice(k * BANK, (k + 1) * BANK)
-                w = ring.tile([P, BANK], F32, name="w")
-                nc.vector.tensor_tensor(out=w[:], in0=dense[k][:], in1=placed_b[:, cols], op=ALU.add)
-                part.append(w)
-            if k > 0:
-                cols = slice((k - 1) * BANK, k * BANK)
-                y = ring.tile([P, BANK], F32, name="y")
-                nc.vector.tensor_tensor(out=y[:], in0=part[k - 1][:], in1=placed_a[:, cols], op=ALU.add)
-                nc.sync.dma_start(out=out[:, cols], in_=y[:])
+            nc.sync.dma_start(out=out[:, cols], in_=y[:])
+
+        for j in range(4):
+            for s, b in enumerate(blocks_of(j)):
+                turn(turned[j][:, s, :], placed_b[:, b * P : (b + 1) * P], False, s == 3)
+            sum_t = keep.tile([P, 4, P], F32, name=f"sum_t{j}")
+            nc.scalar.copy(out=sum_t[:], in_=turned[j][:])
+            sums.append(sum_t)
+        for c in range(6):
+            finish(c)

@@ -21,7 +21,10 @@ AX = mybir.AxisListType
 P = 128
 PACK = 4
 BANK = 512
-BANKS = V // BANK
+WIDTHS = [256,256,512,512,512]
+STARTS = [sum(WIDTHS[:k]) for k in range(len(WIDTHS))]
+PARTS = len(WIDTHS)
+ACC_TAGS = ["acc0","acc1","acc2","acc3","turned0"]
 
 
 def tile_attend_bjointcover_heads_kernel(tc, hid, voc_words, voc_scales, stake, old, offs, offs2, out):
@@ -35,13 +38,15 @@ def tile_attend_bjointcover_heads_kernel(tc, hid, voc_words, voc_scales, stake, 
 
         hid_raw = keep.tile([P, PACK, Q], F32, tag="staging")
         nc.sync.dma_start(out=hid_raw[:], in_=hid.rearrange("(p t) q -> p t q", t=PACK))
-        for quad in range(4):
-            nc.scalar.dma_start(
-                out=planes[32 * quad : 32 * quad + 4, :].bitcast(I32),
-                in_=voc_scales[0, 4 * quad : 4 * quad + 4, :].bitcast(I32),
-            )
-        words = keep.tile([P, 2 * V], U8, align_bytes=64)
-        nc.sync.dma_start(out=words[:].bitcast(I32), in_=voc_words[0].bitcast(I32))
+        scale_rows = voc_scales[0].bitcast(I32).rearrange("(quad r) c -> r quad c", r=4)
+        for r in range(4):
+            queue = nc.sync if r < 2 else nc.scalar
+            queue.dma_start(out=planes[r:P:32, :].bitcast(I32), in_=scale_rows[r])
+        words = []
+        for half in range(2):
+            w = keep.tile([P, V], U8, align_bytes=64, name=f"words{half}")
+            nc.sync.dma_start(out=w[:].bitcast(I32), in_=voc_words[0, :, half * V : (half + 1) * V].bitcast(I32))
+            words.append(w)
         list_a = keep.tile([P, LISTED // 16], U16)
         nc.sync.dma_start(out=list_a[:], in_=offs)
         list_b = keep.tile([P, LISTED // 16], U16)
@@ -73,60 +78,68 @@ def tile_attend_bjointcover_heads_kernel(tc, hid, voc_words, voc_scales, stake, 
 
         a = keep.tile([P, V], F32)
         p = keep.tile([P, V], F32)
-        bank_max = keep.tile([P, BANKS], F32)
-        bank_neg = keep.tile([P, BANKS], F32)
-        bank_sum = keep.tile([P, BANKS], F32)
-        for k in range(BANKS):
-            cols = slice(k * BANK, (k + 1) * BANK)
-            acc = psum.tile([P, BANK], F32, name=f"acc{k}")
+        part_max = keep.tile([P, PARTS], F32)
+        part_neg = keep.tile([P, PARTS], F32)
+        part_sum = keep.tile([P, PARTS], F32)
+        for k, (start, width) in enumerate(zip(STARTS, WIDTHS)):
+            cols = slice(start, start + width)
+            half, at = divmod(2 * start, V)
+            acc = psum.tile([P, width], F32, name=f"acc{k}", tag=ACC_TAGS[k])
             nc.tensor.matmul_mx(
                 out=acc[:],
                 lhsT=codes[:].bitcast(FP8X4),
                 lhsT_scale=hid_plane[:],
-                rhs=words[:, 2 * k * BANK : 2 * (k + 1) * BANK].bitcast(FP4X4),
+                rhs=words[half][:, at : at + 2 * width].bitcast(FP4X4),
                 rhs_scale=planes[:, cols],
                 start=True,
                 stop=True,
             )
             nc.vector.tensor_scalar(
                 out=a[:, cols], in0=acc[:], scalar1=1.0, scalar2=None, op0=ALU.mult, op1=ALU.max,
-                accum_out=bank_max[:, k : k + 1],
+                accum_out=part_max[:, k : k + 1],
             )
-            nc.scalar.mul(bank_neg[:, k : k + 1], bank_max[:, k : k + 1], -1.0)
+            nc.scalar.mul(part_neg[:, k : k + 1], part_max[:, k : k + 1], -1.0)
             nc.scalar.activation(
-                out=p[:, cols], in_=a[:, cols], func=ACT.Exp, bias=bank_neg[:, k : k + 1],
-                accum_out=bank_sum[:, k : k + 1],
+                out=p[:, cols], in_=a[:, cols], func=ACT.Exp, bias=part_neg[:, k : k + 1],
+                accum_out=part_sum[:, k : k + 1],
             )
 
-        got_a = keep.tile([P, LISTED], F32)
-        nc.vector.tensor_copy(out=got_a[:], in_=a[:].indirect(list_a[:]))
         neg_max = keep.tile([P, 1], F32)
-        nc.vector.tensor_reduce(out=neg_max[:], in_=bank_max[:], axis=AX.X, op=ALU.max, negate=True)
-        got_b = keep.tile([P, LISTED], F32)
-        nc.vector.tensor_copy(out=got_b[:], in_=a[:].indirect(list_b[:]))
-
         px_a = keep.tile([P, LISTED], F32)
         sum_a = keep.tile([P, 1], F32)
+        rebase = keep.tile([P, PARTS], F32)
+        got_a = keep.tile([P, LISTED], F32)
+        nc.vector.tensor_copy(out=got_a[:], in_=a[:].indirect(list_a[:]))
+        nc.vector.tensor_reduce(out=neg_max[:], in_=part_max[:], axis=AX.X, op=ALU.max, negate=True)
+        got_b = keep.tile([P, LISTED], F32)
+        nc.vector.tensor_copy(out=got_b[:], in_=a[:].indirect(list_b[:]))
         nc.scalar.activation(out=px_a[:], in_=got_a[:], func=ACT.Exp, bias=neg_max[:], accum_out=sum_a[:])
-        rebase = keep.tile([P, BANKS], F32)
-        nc.scalar.activation(out=rebase[:], in_=bank_max[:], func=ACT.Exp, bias=neg_max[:])
-        coef = keep.tile([P, 1 + BANKS], F32)
-        nc.scalar.mul(coef[:, 0:1], stake_sb[:], 512.0)
-        h = keep.tile([P, 1], F32)
-        nc.scalar.activation(out=h[:], in_=sum_a[:], func=ACT.Copy, scale=coef[:, 0:1])
+        nc.scalar.activation(out=rebase[:], in_=part_max[:], func=ACT.Exp, bias=neg_max[:])
         px_b = keep.tile([P, LISTED], F32)
         sum_b = keep.tile([P, 1], F32)
         nc.scalar.activation(out=px_b[:], in_=got_b[:], func=ACT.Exp, bias=neg_max[:], accum_out=sum_b[:])
 
-        z_parts = keep.tile([P, BANKS], F32)
+        coef = keep.tile([P, 1 + PARTS], F32)
+        nc.scalar.mul(coef[:, 0:1], stake_sb[:], 512.0)
+        z_parts = keep.tile([P, PARTS], F32)
         z = keep.tile([P, 1], F32)
         nc.vector.scalar_tensor_tensor(
-            out=z_parts[:], in0=bank_sum[:], scalar=1.0, in1=rebase[:], op0=ALU.mult, op1=ALU.mult, accum_out=z[:]
+            out=z_parts[:], in0=part_sum[:], scalar=1.0, in1=rebase[:], op0=ALU.mult, op1=ALU.mult, accum_out=z[:]
         )
+        h = keep.tile([P, 1], F32)
+        nc.vector.tensor_tensor(out=h[:], in0=sum_a[:], in1=coef[:, 0:1], op=ALU.mult)
         zz = keep.tile([P, 1], F32)
         nc.vector.scalar_tensor_tensor(out=zz[:], in0=z[:], scalar=0.0625, in1=z[:], op0=ALU.mult, op1=ALU.mult)
         z_inv = keep.tile([P, 1], F32)
         nc.vector.reciprocal(out=z_inv[:], in_=z[:])
+        rebase_h = keep.tile([P, PARTS], F32)
+        nc.vector.tensor_scalar(
+            out=rebase_h[:], in0=rebase[:], scalar1=h[:], scalar2=None, op0=ALU.mult
+        )
+        nc.vector.scalar_tensor_tensor(
+            out=coef[:, 1:], in0=rebase_h[:], scalar=-2.0, in1=z_inv[:].to_broadcast([P, PARTS]),
+            op0=ALU.mult, op1=ALU.mult,
+        )
 
         den = keep.tile([P, 1], F32)
         nc.vector.tensor_scalar(
@@ -138,20 +151,15 @@ def tile_attend_bjointcover_heads_kernel(tc, hid, voc_words, voc_scales, stake, 
         nc.vector.tensor_scalar(
             out=e_b[:], in0=px_b[:], scalar1=h[:], scalar2=den_inv[:], op0=ALU.mult, op1=ALU.mult
         )
+        coef2 = keep.tile([P, 1 + PARTS], F32)
+        nc.vector.tensor_scalar(
+            out=coef2[:], in0=coef[:], scalar1=sum_b[:], scalar2=den_inv[:], op0=ALU.mult, op1=ALU.mult
+        )
         nc.vector.tensor_copy(out=placed_b[:].indirect(list_b[:]), in_=e_b[:])
 
-        hz = keep.tile([P, 1], F32)
-        nc.scalar.activation(out=hz[:], in_=h[:], func=ACT.Copy, scale=z_inv[:])
-        hz2 = keep.tile([P, 1], F32)
-        nc.scalar.mul(hz2[:], hz[:], -2.0)
-        nc.scalar.activation(out=coef[:, 1:], in_=rebase[:], func=ACT.Copy, scale=hz2[:])
-        coef1 = keep.tile([P, 1 + BANKS], F32)
-        nc.scalar.activation(out=coef1[:], in_=coef[:], func=ACT.Copy, scale=sum_b[:])
-        coef2 = keep.tile([P, 1 + BANKS], F32)
-        nc.scalar.activation(out=coef2[:], in_=coef1[:], func=ACT.Copy, scale=den_inv[:])
         u = keep.tile([P, V], F32)
-        for k in range(BANKS):
-            cols = slice(k * BANK, (k + 1) * BANK)
+        for k, (start, width) in enumerate(zip(STARTS, WIDTHS)):
+            cols = slice(start, start + width)
             nc.scalar.activation(out=u[:, cols], in_=p[:, cols], func=ACT.Copy, scale=coef2[:, 1 + k : 2 + k])
         e_a = keep.tile([P, LISTED], F32)
         nc.scalar.activation(out=e_a[:], in_=px_a[:], func=ACT.Copy, scale=coef2[:, 0:1])
@@ -173,7 +181,7 @@ def tile_attend_bjointcover_heads_kernel(tc, hid, voc_words, voc_scales, stake, 
             turn(turned[j][:, s, :], u[:, b * P : (b + 1) * P], False, False)
 
         sums = []
-        chunks = [[0, 1, 2], [3, 4, 5], [6, 7, 8], [9, 10, 11], [12, 13], [14, 15]]
+        chunks = [[0,1,2],[3,4,5],[6,7,8],[9,10,11],[12,13,14],[15]]
         tags = ["acc0", "acc1", "acc2", "acc3", "turned0", "turned1"]
 
         def finish(c):

from contextlib import ExitStack

import concourse.mybir as mybir
from concourse.masks import make_identity

D, V, Q, LISTED = 512, 2048, 128, 512
FLOPS = 2 * D * V * Q

F32 = mybir.dt.float32
BF16 = mybir.dt.bfloat16
I32 = mybir.dt.int32
U32 = mybir.dt.uint32
U16 = mybir.dt.uint16
U8 = mybir.dt.uint8
FP8X4 = mybir.dt.float8_e4m3fn_x4
FP4X4 = mybir.dt.float4_e2m1fn_x4
ALU = mybir.AluOpType
ACT = mybir.ActivationFunctionType
AX = mybir.AxisListType

P = 128
PACK = 4
BANK = 512
WIDTHS = [256,256,512,512,512]
STARTS = [sum(WIDTHS[:k]) for k in range(len(WIDTHS))]
PARTS = len(WIDTHS)
ACC_TAGS = ["acc0","acc1","acc2","acc3","turned0"]


def tile_attend_bjointcover_heads_kernel(tc, hid, voc_words, voc_scales, stake, old, offs, offs2, out):
    nc = tc.nc
    with ExitStack() as ctx:
        keep = ctx.enter_context(tc.tile_pool(name="keep", bufs=1))
        psum = ctx.enter_context(tc.psum_pool(name="psum", bufs=1))

        planes = keep.tile([P, V], U8, align_bytes=64)
        nc.vector.memset(planes[:].bitcast(U32), 0)

        hid_raw = keep.tile([P, PACK, Q], F32, tag="staging")
        nc.sync.dma_start(out=hid_raw[:], in_=hid.rearrange("(p t) q -> p t q", t=PACK))
        scale_rows = voc_scales[0].bitcast(I32).rearrange("(quad r) c -> r quad c", r=4)
        for r in range(4):
            queue = nc.sync if r < 2 else nc.scalar
            queue.dma_start(out=planes[r:P:32, :].bitcast(I32), in_=scale_rows[r])
        words = []
        for half in range(2):
            w = keep.tile([P, V], U8, align_bytes=64, name=f"words{half}")
            nc.sync.dma_start(out=w[:].bitcast(I32), in_=voc_words[0, :, half * V : (half + 1) * V].bitcast(I32))
            words.append(w)
        list_a = keep.tile([P, LISTED // 16], U16)
        nc.sync.dma_start(out=list_a[:], in_=offs)
        list_b = keep.tile([P, LISTED // 16], U16)
        nc.sync.dma_start(out=list_b[:], in_=offs2)

        placed_b = keep.tile([P, V], F32)
        nc.vector.memset(placed_b[:], 0.0)
        stake_sb = keep.tile([P, 1], F32)
        nc.gpsimd.dma_start(out=stake_sb[:], in_=stake)

        ident = keep.tile([P, P], F32)
        make_identity(nc, ident[:])

        grouped = keep.tile([P, Q, PACK], BF16, align_bytes=64, tag="grouped")
        nc.vector.tensor_copy(
            out=grouped[:].rearrange("p (c i) t -> p c t i", i=4),
            in_=hid_raw[:].rearrange("p t (c i) -> p c t i", i=4),
        )
        codes = keep.tile([P, Q], U32, align_bytes=64)
        hid_plane = keep.tile([P, Q], U8, align_bytes=64)
        nc.vector.quantize_mx(
            out=codes[:].bitcast(FP8X4), scales=hid_plane[:], in_=grouped[:].rearrange("p q t -> p (q t)")
        )

        old_sb = keep.tile([P, V], F32, tag="staging")
        nc.sync.dma_start(out=old_sb[:], in_=old)
        placed_a = keep.tile([P, V], F32, align_bytes=64, tag="grouped")
        nc.gpsimd.memset(placed_a[:], 0.0)

        a = keep.tile([P, V], F32)
        p = keep.tile([P, V], F32)
        part_max = keep.tile([P, PARTS], F32)
        part_neg = keep.tile([P, PARTS], F32)
        part_sum = keep.tile([P, PARTS], F32)
        for k, (start, width) in enumerate(zip(STARTS, WIDTHS)):
            cols = slice(start, start + width)
            half, at = divmod(2 * start, V)
            acc = psum.tile([P, width], F32, name=f"acc{k}", tag=ACC_TAGS[k])
            nc.tensor.matmul_mx(
                out=acc[:],
                lhsT=codes[:].bitcast(FP8X4),
                lhsT_scale=hid_plane[:],
                rhs=words[half][:, at : at + 2 * width].bitcast(FP4X4),
                rhs_scale=planes[:, cols],
                start=True,
                stop=True,
            )
            nc.vector.tensor_scalar(
                out=a[:, cols], in0=acc[:], scalar1=1.0, scalar2=None, op0=ALU.mult, op1=ALU.max,
                accum_out=part_max[:, k : k + 1],
            )
            nc.scalar.mul(part_neg[:, k : k + 1], part_max[:, k : k + 1], -1.0)
            nc.scalar.activation(
                out=p[:, cols], in_=a[:, cols], func=ACT.Exp, bias=part_neg[:, k : k + 1],
                accum_out=part_sum[:, k : k + 1],
            )

        neg_max = keep.tile([P, 1], F32)
        px_a = keep.tile([P, LISTED], F32)
        sum_a = keep.tile([P, 1], F32)
        rebase = keep.tile([P, PARTS], F32)
        got_a = keep.tile([P, LISTED], F32)
        nc.vector.tensor_copy(out=got_a[:], in_=a[:].indirect(list_a[:]))
        nc.vector.tensor_reduce(out=neg_max[:], in_=part_max[:], axis=AX.X, op=ALU.max, negate=True)
        got_b = keep.tile([P, LISTED], F32)
        nc.vector.tensor_copy(out=got_b[:], in_=a[:].indirect(list_b[:]))
        nc.scalar.activation(out=px_a[:], in_=got_a[:], func=ACT.Exp, bias=neg_max[:], accum_out=sum_a[:])
        nc.scalar.activation(out=rebase[:], in_=part_max[:], func=ACT.Exp, bias=neg_max[:])
        px_b = keep.tile([P, LISTED], F32)
        sum_b = keep.tile([P, 1], F32)
        nc.scalar.activation(out=px_b[:], in_=got_b[:], func=ACT.Exp, bias=neg_max[:], accum_out=sum_b[:])

        coef = keep.tile([P, 1 + PARTS], F32)
        nc.scalar.mul(coef[:, 0:1], stake_sb[:], 512.0)
        z_parts = keep.tile([P, PARTS], F32)
        z = keep.tile([P, 1], F32)
        nc.vector.scalar_tensor_tensor(
            out=z_parts[:], in0=part_sum[:], scalar=1.0, in1=rebase[:], op0=ALU.mult, op1=ALU.mult, accum_out=z[:]
        )
        h = keep.tile([P, 1], F32)
        nc.vector.tensor_tensor(out=h[:], in0=sum_a[:], in1=coef[:, 0:1], op=ALU.mult)
        zz = keep.tile([P, 1], F32)
        nc.vector.scalar_tensor_tensor(out=zz[:], in0=z[:], scalar=0.0625, in1=z[:], op0=ALU.mult, op1=ALU.mult)
        z_inv = keep.tile([P, 1], F32)
        nc.vector.reciprocal(out=z_inv[:], in_=z[:])
        rebase_h = keep.tile([P, PARTS], F32)
        nc.vector.tensor_scalar(
            out=rebase_h[:], in0=rebase[:], scalar1=h[:], scalar2=None, op0=ALU.mult
        )
        nc.vector.scalar_tensor_tensor(
            out=coef[:, 1:], in0=rebase_h[:], scalar=-2.0, in1=z_inv[:].to_broadcast([P, PARTS]),
            op0=ALU.mult, op1=ALU.mult,
        )

        den = keep.tile([P, 1], F32)
        nc.vector.tensor_scalar(
            out=den[:], in0=sum_b[:], scalar1=sum_a[:], scalar2=zz[:], op0=ALU.mult, op1=ALU.add
        )
        den_inv = keep.tile([P, 1], F32)
        nc.vector.reciprocal(out=den_inv[:], in_=den[:])
        e_b = keep.tile([P, LISTED], F32)
        nc.vector.tensor_scalar(
            out=e_b[:], in0=px_b[:], scalar1=h[:], scalar2=den_inv[:], op0=ALU.mult, op1=ALU.mult
        )
        coef2 = keep.tile([P, 1 + PARTS], F32)
        nc.vector.tensor_scalar(
            out=coef2[:], in0=coef[:], scalar1=sum_b[:], scalar2=den_inv[:], op0=ALU.mult, op1=ALU.mult
        )
        nc.vector.tensor_copy(out=placed_b[:].indirect(list_b[:]), in_=e_b[:])

        u = keep.tile([P, V], F32)
        for k, (start, width) in enumerate(zip(STARTS, WIDTHS)):
            cols = slice(start, start + width)
            nc.scalar.activation(out=u[:, cols], in_=p[:, cols], func=ACT.Copy, scale=coef2[:, 1 + k : 2 + k])
        e_a = keep.tile([P, LISTED], F32)
        nc.scalar.activation(out=e_a[:], in_=px_a[:], func=ACT.Copy, scale=coef2[:, 0:1])
        nc.vector.tensor_copy(out=placed_a[:].indirect(list_a[:]), in_=e_a[:])

        def blocks_of(j):
            return [3 * j, 3 * j + 1, 3 * j + 2, 12 + j]

        def turn(dst, src, start, stop):
            nc.tensor.matmul(out=dst, lhsT=src, rhs=ident[:], is_transpose=True, start=start, stop=stop)

        turned = [psum.tile([P, 4, P], F32, name=f"turned{j}") for j in range(4)]
        place = {b: (j, s) for j in range(4) for s, b in enumerate(blocks_of(j))}
        for b in range(16):
            j, s = place[b]
            turn(turned[j][:, s, :], old_sb[:, b * P : (b + 1) * P], s == 0, False)
        for b in range(16):
            j, s = place[b]
            turn(turned[j][:, s, :], u[:, b * P : (b + 1) * P], False, False)

        sums = []
        chunks = [[0,1,2],[3,4,5],[6,7,8],[9,10,11],[12,13,14],[15]]
        tags = ["acc0", "acc1", "acc2", "acc3", "turned0", "turned1"]

        def finish(c):
            blocks = chunks[c]
            back = psum.tile([P, len(blocks), P], F32, name=f"back{c}", tag=tags[c])
            for i, b in enumerate(blocks):
                j, s = place[b]
                turn(back[:, i, :], sums[j][:, s, :], True, True)
            cols = slice(blocks[0] * P, (blocks[-1] + 1) * P)
            y = keep.tile([P, len(blocks) * P], F32, name=f"y{c}")
            nc.vector.tensor_tensor(
                out=y[:], in0=placed_a[:, cols], in1=back[:].rearrange("p i q -> p (i q)"), op=ALU.add
            )
            nc.sync.dma_start(out=out[:, cols], in_=y[:])

        for j in range(4):
            for s, b in enumerate(blocks_of(j)):
                turn(turned[j][:, s, :], placed_b[:, b * P : (b + 1) * P], False, s == 3)
            sum_t = keep.tile([P, 4, P], F32, name=f"sum_t{j}")
            nc.scalar.copy(out=sum_t[:], in_=turned[j][:])
            sums.append(sum_t)
        for c in range(6):
            finish(c)
